import numpy as np, ml_dtypes
CORES = [36,164,52,180,100,228,116,244]
N = 8
import mx_ref
BF = ml_dtypes.bfloat16
def gentries(a):
    return np.ascontiguousarray(a.reshape(8, 16, -1).transpose(0, 2, 1)).reshape(8, -1)
def gtable(e):
    e = np.asarray(e); return np.ascontiguousarray(e.reshape(8, -1, 16).transpose(0, 2, 1)).reshape(128, -1).astype(np.int32)
def gcols(t, e):
    v = np.concatenate([t.reshape(8, 16, -1, 4), np.zeros((8, 16, 1, 4), BF)], axis=2)
    return np.ascontiguousarray(np.stack([v[g][:, e[g]] for g in range(8)])).reshape(128, -1)
def gpick(z, e):
    return np.concatenate([z[16 * g:16 * g + 16][:, e[g]] for g in range(8)])
def tile(rs):
    return np.stack(rs, axis=2).reshape(128, -1).astype(BF)
def pick(q, e):
    c = np.concatenate([q[0].reshape(128, -1, 4), np.zeros((128, 1, 4), np.uint8)], axis=1); s = np.concatenate([q[1], np.ones((16, 1), np.uint8)], axis=1)
    return (np.ascontiguousarray(c[:, e].reshape(128, -1)), np.ascontiguousarray(s[:, e]))
def join(*qs):
    return (np.concatenate([q[0] for q in qs], axis=1), np.concatenate([q[1] for q in qs], axis=1))
def put(q, e, v):
    c, s = q[0].reshape(128, -1, 4).copy(), q[1].copy(); c[:, e] = v[0].reshape(128, -1, 4); s[:, e] = v[1]
    return (c.reshape(128, -1), s)
def pk(c, s):
    return (np.ascontiguousarray(c), mx_ref.live(s))
def emit(q):
    return q[0], q[1]
def packed(v, rng):
    q = [mx_ref.quantize(np.ascontiguousarray(v[r])) for r in range(N)]
    return np.stack([a for a, b in q]), np.stack([mx_ref.plane(b, rng) for a, b in q])
def f(rng, *shape):
    return mx_ref.flush((rng.standard_normal(shape, dtype=np.float32) * np.exp2(rng.integers(-2, 3, shape[:-1] + (1,)))).astype(BF))
def wide(rng, *shape, cols=0):
    v = rng.standard_normal(shape, dtype=np.float32) * np.exp2(rng.integers(-12, 13, shape)).astype(np.float32)
    if cols: v *= np.repeat(np.exp2(rng.integers(-cols, cols + 1, shape[:-2] + (1, shape[-1] // 4))) * (rng.random(shape[:-2] + (1, shape[-1] // 4)) > 0.0625), 4, axis=-1).astype(np.float32)
    return mx_ref.flush(v.astype(BF))
C, R = 288, 3
def big(v):
    v = v.astype(np.float32)
    v[np.abs(v) < np.float32(2.0 ** -16)] = 0
    return v.astype(BF)
def numbers_of(rng):
    return {"x": big(f(rng, N, 128, 4 * C)), "u": np.array(f(rng, N, 128, 512)), "v": np.array(f(rng, N, 128, 512))}
def lookups(e):
    return {"ct": np.stack([gtable(e[r]) for r in range(N)])}
def any_lookups(rng):
    return rng.integers(0, 16, (N, 8, 256))
def layers(rng):
    return big(f(rng, N, 128, 2048)).reshape(N, 8, 16, 4, 8, 16, 4)
def weights(rng, w):
    c, p = packed(np.ascontiguousarray(w).reshape(N, 128, 2048), rng)
    return {"wc": c, "ws": p}
def signs(c):
    return ((c[:, :, None] >> np.arange(3, -1, -1)[:, None]) & 1) * 2.0 - 1.0
def single(d, k):
    u = d["u"].reshape(N, 128, 128, 4)
    for b in range(4):
        u[:, :, b::16] = 0
        for h in range(0, 128, 16): u[:, h + b, h + b, 0] = k
    return u
def setup_inputs(rng):
    return {**numbers_of(rng), **lookups(any_lookups(rng)), **weights(rng, layers(rng))}
def setup_inputs_near(rng):
    d = numbers_of(rng)
    x = d["x"].reshape(N, 8, 16, C, 4)
    o = rng.permutation(N) % 4
    k = np.where(o < 2, 2.0 ** -30, 1.0)
    u = single(d, k.astype(np.float32).astype(BF))
    x[:, :, :8] = 0
    for r in range(N):
        s = rng.integers(-1, 2, (8, 4, C)) * k[r]
        for g in rng.permutation(8)[:4]: s[g, :, rng.integers(C)] = 2.0 ** 29 * rng.choice([-1.0, 1.0], 4)
        two = o[r] in (0, 3)
        x[r, :, :4, :, 0] = (s * (1.125 if two else 1.0)).astype(np.float32).astype(BF)
        if two:
            x[r, :, 4:8, :, 0] = (-s).astype(np.float32).astype(BF)
            for h in range(0, 128, 16):
                for b in range(4):
                    u[r, h + b, h + b, 0] = 1.125 * k[r]
                    u[r, h + 4 + b, h + b, 0] = 1.25 * k[r]
    w = layers(rng)
    w[:, :, :8] = 0
    w[:, :, :, :, :, :8] = 0
    return {"x": x.reshape(N, 128, 4 * C), "u": u.reshape(N, 128, 512), "v": d["v"], **lookups(any_lookups(rng)), **weights(rng, w)}
def setup_inputs_late(rng):
    d = numbers_of(rng)
    x = d["x"].reshape(N, 8, 16, C, 4)
    c = (rng.permutation(N) % 2 * 2.0 - 1.0).astype(np.float32).astype(BF)
    x[:, :, 0] = c[:, None, None, None]
    u = d["u"].reshape(N, 128, 128, 4)
    for b in range(4):
        u[:, :, b::16] = 0
        for h in range(0, 128, 16): u[:, h, h + b, b] = 1
    return {"x": x.reshape(N, 128, 4 * C), "u": u.reshape(N, 128, 512), "v": d["v"], **lookups(any_lookups(rng)), **weights(rng, layers(rng))}
def setup_inputs_one(rng):
    d = numbers_of(rng)
    x = d["x"].reshape(N, 8, 16, C, 4)
    c, e, n = rng.integers(0, 16, (N, 8, C)), any_lookups(rng), np.arange(256)
    for r in rng.permutation(N)[:N // 2]:
        a = (rng.integers(C) - np.arange(C)) % C
        h = np.arange(8)[:, None] % 2
        c[r] = np.where(a < 256, np.where(h == 0, a // 16, a % 16), c[r])
        e[r] = np.where(h == 0, n // 16, n % 16)
        e[r, 7] = n // 16
    x[:, :, :8] = 0
    x[:, :, :4, :, 0] = signs(c).astype(np.float32).astype(BF)
    u = single(d, np.ones(N, np.float32).astype(BF))
    w = layers(rng)
    w[:, :, :, :, :, :8] = 0
    return {"x": x.reshape(N, 128, 4 * C), "u": u.reshape(N, 128, 512), "v": d["v"], **lookups(e), **weights(rng, w)}
def setup_inputs_ends(rng):
    d = numbers_of(rng)
    o = rng.permutation(N) % 4
    u = single(d, np.where(o == 1, 2.0 ** -30, 2.0 ** 30).astype(np.float32).astype(BF))
    x = 2.0 ** 30 * (0.75 + 0.1 * rng.random((N, 8, 16, C, 4))) * rng.choice([-1.0, 1.0], (N, 8, 1, C, 1))
    x[:, :, :8] = 0
    x[:, :, :4, :, 0] = signs(rng.integers(0, 16, (N, 8, C))) * 2.0 ** 30
    e = rng.integers(0, 2, (N, 8, 256)) * 15
    w = np.zeros((N, 128, 4, 128, 4), np.float32)
    i = np.arange(128)
    i = i[i % 16 >= 8]
    for r in range(N):
        if o[r] == 0:
            x[r] = 2.0 ** 30 * rng.choice([-1.0, 1.0], (1, 1, C, 1))
            for b in range(4): u[r][:, b::16] = (2.0 ** 30 * rng.choice([-1.0, 1.0], (1, 8, 1)) * np.ones((128, 1, 4))).astype(np.float32).astype(BF)
            e[r] = 15
        if o[r] == 1:
            x[r, :, :4] *= 2.0 ** -60
            x[r, :, 8:] = 2.0 ** -30 * rng.choice([-1.0, 1.0], (8, 8, C, 4))
            e[r] = 0
        if o[r] == 2: x[r, :, :8] = 0
        if o[r] == 3: e[r] = rng.integers(0, 2, (8, 1)) * 15
        if o[r] >= 2:
            for b in range(4): w[r, i, b, i, b] = rng.choice([-1.0, 1.0], len(i))
    d["v"] = (np.where(d["v"] < 0, -1.0, 1.0) * np.where(rng.permutation(N) % 2, 2.0 ** -30, 2.0 ** 30)[:, None, None]).astype(np.float32).astype(BF)
    return {"x": x.astype(np.float32).reshape(N, 128, 4 * C).astype(BF), "u": u.reshape(N, 128, 512), "v": d["v"], **lookups(e), **weights(rng, w.astype(BF))}
def setup_inputs_spread(rng):
    d = setup_inputs(rng)
    d["x"] = big(wide(rng, N, 128, 4 * C, cols=6))
    return d
def check_inputs(d):
    b = []
    for k in ("x", "u", "v"):
        a = np.abs(d[k].astype(np.float32))
        if not (np.isfinite(a).all() and ((a == 0) | (a >= 2.0 ** -30) & (a <= 2.0 ** 30)).all()): b.append("a value of " + k)
    if not ((d["ct"] >= 0) & (d["ct"] < 16)).all(): b.append("an entry of ct")
    none, least, most = [emit(mx_ref.quantize(np.full((128, 16), k, np.float32).astype(BF)))[1][0, 0] for k in (0.0, 2.0 ** -30, 2.0 ** 30)]
    for r in range(N):
        if ((d["wc"][r] == 0x7F) | (d["wc"][r] == 0xFF)).any(): b.append("wc: a code that is no number")
        s = mx_ref.live(d["ws"][r])
        if ((s != none) & ((s < least) | (s > most))).any(): b.append("ws: a scale out of range")
    return b
def reference(x, u, v, ct, wc, ws):
    qu = [mx_ref.quantize(u[r]) for r in range(N)]
    lay = [pk(wc[r], ws[r]) for r in range(N)]
    now = [x[r] for r in range(N)]
    k = [gentries(ct[r]) for r in range(N)]
    for t in range(R):
        place, z = [], []
        for r in range(N):
            s = (mx_ref.matmul(qu[r], mx_ref.quantize(now[r])) > 0).astype(np.int64)
            c = 8 * s[::16] + 4 * s[1::16] + 2 * s[2::16] + s[3::16]
            a = np.zeros((8, C), np.int64)
            a[:4] = 16 * c[::2] + c[1::2]
            a[4] = 16 * k[r][0][a[0]] + k[r][1][a[1]]
            a[5] = 16 * k[r][2][a[2]] + k[r][3][a[3]]
            a[6] = 16 * k[r][4][a[4]] + k[r][5][a[5]]
            a[7] = 16 * k[r][6][a[6]] + k[r][7][16 * c[7] + c[0]]
            place.append((a + np.arange(C)) % C)
            z.append(mx_ref.quantize(gcols(now[r], place[r])))
        made = []
        for r in range(N):
            q, e = z[(r - 1 - t) % N], place[r][[1, 0, 3, 2, 5, 4, 7, 6]]
            made.append(tile([gpick(mx_ref.matmul(pick(lay[r], np.arange(128 * b, 128 * b + 128)), q) * np.float32(0.03125), e) + now[r][:, b::4].astype(np.float32) for b in range(4)]))
        now = made
    y, lo = np.zeros((N, 128, C), np.float32), np.zeros((N, 8, C), np.float32)
    oc, osc = np.zeros((N, 128, 4 * C), np.uint8), np.zeros((N, 16, C), np.uint8)
    for r in range(N):
        q = mx_ref.quantize(now[r])
        y[r] = mx_ref.matmul(mx_ref.quantize(v[r]), q)
        lo[r] = place[r]
        oc[r], osc[r] = emit(q)
    return {"y": y, "lo": lo, "oc": oc, "osc": osc}

@@ -1,0 +1,333 @@
+from concourse.mybir import dt, AluOpType, ActivationFunctionType
+
+C, R = 288, 3
+EXT = 544
+F8, U8 = "float8_e4m3fn_x4", "uint8"
+IDN, Q0, Q3, Q2, ZERO = 0, 512, 1536, 2048, 2560
+FE, FV, FA, FL = 30, 36, 108, 160
+S1, S0 = 12, 32
+FBASE = (FV, FV - S0 + 6, FA - S1, FL)
+
+SCRATCH = {
+    "xp": ("sbuf", [128, 4 * EXT], "bfloat16"),
+    "z": ("sbuf", [128, 4 * C], "bfloat16"),
+    "ut": ("sbuf", [128, 512], "bfloat16"),
+    "vt": ("sbuf", [128, 512], "bfloat16"),
+    "zt": ("sbuf", [128, 512], "bfloat16"),
+    "qu": ("sbuf", [128, 128], F8), "su": ("sbuf", [128, 128], U8),
+    "qu2": ("sbuf", [128, 128], F8), "su2": ("sbuf", [128, 128], U8),
+    "qv": ("sbuf", [128, 128], F8), "sv": ("sbuf", [128, 128], U8),
+    "qw": ("sbuf", [128, 512], F8), "sw": ("sbuf", [128, 512], U8),
+    "qx": ("sbuf", [128, 384], F8), "sx": ("sbuf", [128, 384], U8),
+    "cts": ("sbuf", [128, 64], "int32"),
+    "inb": ("sbuf", [128, 2048], "bfloat16"),
+    "tab": ("sbuf", [128, ZERO + 16], "bfloat16"),
+    "ci": ("sbuf", [128, 224], "float32"),
+    "co": ("sbuf", [128, 224], "float32"),
+    "col": ("sbuf", [128, 8], "float32"),
+    "j0": ("sbuf", [128, 18], "float32"),
+    "jt": ("sbuf", [128, 18], "float32"),
+    "im": ("sbuf", [128, EXT], "float32"),
+    "mul": ("sbuf", [128, 120], "float32"),
+    "sg": ("sbuf", [128, 120], "float32"),
+    "sc": ("sbuf", [128, 120], "float32"),
+    "offu": ("sbuf", [128, 8], "uint16"),
+    "lp": ("sbuf", [128, 2], "uint16"),
+    "lf": ("sbuf", [128, 2], "uint16"),
+    "off1": ("sbuf", [128, 12], "uint16"),
+    "off2": ("sbuf", [128, 6], "uint16"),
+    "off3": ("sbuf", [128, 6], "uint16"),
+    "offp": ("sbuf", [128, 22], "uint16"),
+    "offz": ("sbuf", [128, 32], "uint16"),
+    "offg": ("sbuf", [128, 18], "uint16"),
+    "g1": ("sbuf", [128, 192], "bfloat16"), "t1": ("sbuf", [128, 192], "bfloat16"),
+    "g2": ("sbuf", [128, 96], "bfloat16"), "t2": ("sbuf", [128, 96], "bfloat16"),
+    "g3": ("sbuf", [128, 96], "bfloat16"), "t3": ("sbuf", [128, 96], "bfloat16"),
+    "gp": ("sbuf", [128, 288], "bfloat16"), "tp": ("sbuf", [128, 288], "bfloat16"),
+    "a45": ("sbuf", [128, 6], "float32"), "a45v": ("sbuf", [128, 6], "float32"),
+    "f": ("sbuf", [128, 224], "float32"),
+    "ld": ("sbuf", [128, 64], "float32"), "lt": ("sbuf", [128, 64], "float32"),
+    "ls": ("sbuf", [128, 32], "float32"), "lm": ("sbuf", [128, 18], "float32"), "ln": ("sbuf", [128, 18], "float32"),
+    "lrow": ("sbuf", [128, C], "float32"),
+    "h": ("sbuf", [128, 4 * C], "float32"),
+    "yb": ("sbuf", [128, C], "float32"),
+    "psw": ("psum", [128, 1536], "float32"),
+    "psh": ("psum", [128, 2048], "float32"),
+    "psy": ("psum", [128, 512], "float32"),
+}
+for _t in range(R + 1):
+    SCRATCH["x%d" % _t] = ("sbuf", [128, 4 * C], "bfloat16")
+for _t in range(R):
+    SCRATCH["qz%d" % _t] = ("sbuf", [128, C], F8)
+    SCRATCH["sz%d" % _t] = ("sbuf", [128, C], U8)
+    SCRATCH["ql%d" % _t] = ("sbuf", [128, C], F8)
+    SCRATCH["sl%d" % _t] = ("sbuf", [128, C], U8)
+
+SEMAPHORES = (
+    ["d_x", "d_u", "d_v", "d_w", "d_ct", "d_out", "sent", "arr0", "arr1", "arr2"]
+    + ["m_ci", "m_inb", "m_zt", "m_mul", "m_mul2", "m_misc", "m_fb", "i_a", "i_b", "i_j", "i_id", "i_im", "t_a", "t_b",
+       "k_col", "k_offu", "k_l", "k_j", "q_pad", "q_u", "q_v", "p_uc", "p_us", "c_b1", "c_b2", "c_in", "t_h1", "t_h2"]
+    + ["qx", "mw0", "mw1", "mw2", "sg", "sc", "off1", "g1", "t1", "a45", "off2", "g2", "t2", "off3", "g3", "t3",
+       "fin", "offz", "offp", "gp", "tp", "vv", "a45v", "a45j", "mva1", "mva2", "mvv1", "mvv2",
+       "xm0", "xm1", "xm2", "xm3", "xe_g", "xe_a", "zg_v", "zg_a", "qz", "ld", "lt", "ls", "lm", "ln", "offg",
+       "mh0", "mh1", "mh2", "mh3", "h0", "h1", "h2", "h3", "xn", "lrow", "my", "yb"]
+)
+
+
+def rank_program(g, core, T, topo):
+    rank = T.rank_of(core)
+    if rank is None:
+        return
+    N = len(T.cores)
+    V, A, PE, SY = g.vector, g.scalar, g.tensor, g.sync
+    Q = {"v": V, "a": A, "t": PE, "s": SY, "g": g}
+    add, mult, sub = AluOpType.add, AluOpType.mult, AluOpType.subtract
+    Copy = ActivationFunctionType.Copy
+    cnt = {}
+    seen = {}
+    most = {}
+
+    def wait(q, *names):
+        for n in names:
+            c = cnt[n]
+            if seen.get((q, n), 0) < c:
+                Q[q].wait_ge(T.sem[n], c)
+                seen[(q, n)] = c
+                most[n] = max(most.get(n, 0), c)
+
+    def done(ins, name, k=1):
+        ins.then_inc(T.sem[name], k)
+        cnt[name] = cnt.get(name, 0) + k
+
+    def ts(out, in0, s1, op0, s2=None, op1=None):
+        if op1 is None:
+            return V.tensor_scalar(out, in0, s1, None, op0)
+        return V.tensor_scalar(out, in0, s1, s2, op0, op1)
+
+    def iota(out, pattern, base, cm=0):
+        return g.iota(out, pattern, base, cm, allow_small_or_imprecise_dtypes=True)
+
+    done(SY.dma_start(T.x0[:], T.x[:]), "d_x", 16)
+    done(A.dma_start(T.ut[:], T.u[:]), "d_u", 16)
+    for i, q in enumerate((0, 1, 3, 2)):
+        done(A.dma_start(T.cts[0:32, 16 * i:16 * i + 16], T.ct[32 * q:32 * q + 32, :]), "d_ct", 16)
+    done(SY.dma_start(T.qw[:].bitcast(dt.uint8), T.wc[:]), "d_w", 16)
+    done(SY.dma_start(T.sw[:], T.ws[:]), "d_w", 16)
+    done(SY.dma_start(T.vt[:], T.v[:]), "d_v", 16)
+
+    done(iota(T.ci[:, 0:32], [[0, 2], [16, 4], [1, 4]], 0), "i_a")
+    done(iota(T.ci[:, 32:64], [[0, 2], [16, 4], [1, 4]], 64), "i_a")
+    done(iota(T.ci[:, 64:96], [[0, 4], [-112, 2], [1, 4]], 112), "i_a")
+    done(iota(T.ci[:, 96:128], [[1, 2], [0, 16]], 0), "i_a")
+    done(V.memset(T.ci[:, 128:160], 0.0), "m_ci")
+    done(V.memset(T.zt[:], 0.0), "m_zt")
+    done(V.memset(T.mul[:], 2.0), "m_mul")
+    done(V.memset(T.inb[:], 0.0), "m_inb")
+    wait("g", "m_ci")
+    for h in range(2):
+        done(iota(T.ci[:, 128 + 16 * h:140 + 16 * h], [[16, 2], [40, 3], [8, 2]], 7), "i_b")
+        for s in range(2):
+            done(iota(T.ci[:, 160 + 16 * h + 8 * s:168 + 16 * h + 8 * s], [[S1, 2], [S0, 2], [1, 2]], 2 * s), "i_b")
+    done(iota(T.ci[:, 192:224], [[0, 16], [1, 2]], 4), "i_b")
+    done(iota(T.j0[:], [[0, 3], [128, 3], [16, 2]], 0, 1), "i_j")
+    done(iota(T.tab[:, IDN:IDN + 512], [[16, 16], [0, 2], [1, 16]], 0), "i_id")
+
+    wait("v", "m_zt", "m_mul")
+    done(V.quantize_mx(T.qx[:, 256:384], T.sx[:, 256:384], T.zt[:]), "q_pad")
+    done(V.memset(T.mul[:, 0:120:8], 0.0), "m_mul2")
+    done(V.memset(T.mul[:, 4:120:8], 4.0), "m_mul2")
+    done(V.memset(T.f[:], 0.0), "m_misc")
+    done(V.memset(T.tab[:, ZERO:ZERO + 16], 0.0), "m_misc")
+    done(V.memset(T.offp[:, 0:6:2], ZERO), "m_misc")
+    done(V.memset(T.offu[:, 3:8], 0), "k_offu")
+    for b in range(4):
+        done(V.memset(T.col[32 * b:32 * b + 32, 4:5], float(FBASE[b])), "m_fb")
+    wait("v", "i_a")
+    done(V.transpose(T.co[:, 0:128], T.ci[:, 0:128]), "t_a")
+    wait("v", "t_a")
+    done(V.tensor_copy(T.offu[:, 0:3], T.co[:, 0:96:32]), "k_offu")
+    odd = T.co[:, 96:97]
+    done(ts(T.col[:, 0:1], odd, 16.0, mult), "k_col")
+    done(ts(T.col[:, 1:2], odd, -31.0, mult, 32.0, add), "k_col")
+    done(ts(T.col[:, 2:3], odd, -15.0, mult, 16.0, add), "k_col")
+    done(ts(T.col[:, 3:4], odd, -float(Q3), mult, float(Q3), add), "k_col")
+    h16, sA, sB, bB, fb = (T.col[:, i:i + 1] for i in range(5))
+
+    wait("v", "d_u")
+    done(V.quantize_mx(T.qu[:], T.su[:], T.ut[:]), "q_u")
+    wait("v", "d_ct")
+    done(V.tensor_copy(T.cts[32:64, :], T.cts[0:32, :]), "c_b1")
+    wait("v", "q_u", "k_offu")
+    done(V.tensor_copy(T.qu2[:].bitcast(dt.uint32), T.qu[:].bitcast(dt.uint32).indirect(T.offu[:])), "p_uc")
+    wait("a", "q_u", "k_offu")
+    done(A.activation(T.su2[:], T.su[:].indirect(T.offu[:]), Copy), "p_us")
+    wait("v", "c_b1")
+    done(V.tensor_copy(T.cts[64:128, :], T.cts[0:64, :]), "c_b2")
+    wait("v", "c_b2", "k_col", "m_inb")
+    for i in (0, 16):
+        done(ts(T.inb[:, i:2048:32], T.cts[:], sA, mult), "c_in")
+        done(ts(T.inb[:, i + 8:1536:32], T.cts[:, 0:48], sB, mult), "c_in")
+        done(ts(T.inb[:, 1536 + i + 8:2048:32], T.cts[:, 48:64], sA, mult, bB, add), "c_in")
+
+    for t in range(R):
+        X, XN = T["x%d" % t], T["x%d" % (t + 1)]
+        QZ, SZ, QL, SL = (T[n % t] for n in ("qz%d", "sz%d", "ql%d", "sl%d"))
+        ready = "d_x" if t == 0 else "xn"
+
+        wait("v", ready, "q_pad")
+        done(V.quantize_mx(T.qx[:, 0:C], T.sx[:, 0:C], X[:]), "qx")
+        wait("t", "qx", "p_uc", "p_us")
+        for s in range(3):
+            done(PE.matmul_mx(T.psw[:, 512 * s:512 * s + 128], T.qx[:, 128 * s:128 * s + 128],
+                              T.sx[:, 128 * s:128 * s + 128], T.qu2[:], T.su2[:], True, True), "mw%d" % s)
+        wait("a", ready)
+        for b in range(4):
+            done(A.activation(T.xp[:, EXT * b:EXT * b + C], X[:, b:4 * C:4], Copy), "xm%d" % (b // 2 * 2))
+        done(A.activation(T.xp[:, EXT * 2 + C:EXT * 3], X[:, 2:1024:4], Copy), "xe_a")
+        wait("g", ready)
+        for b in range(2):
+            done(g.affine_select(T.xp[:, EXT * b + C:EXT * (b + 1)], X[:, b:1024:4], [[0, 256]],
+                                 AluOpType.is_ge, 0.0, 0, 0), "xe_g")
+        if t == 0:
+            wait("v", "c_in")
+            done(V.transpose(T.tab[:, Q0:Q0 + 1024], T.inb[:, 0:1024]), "t_h1")
+            wait("v", "i_b")
+            done(V.transpose(T.co[:, 128:224], T.ci[:, 128:224]), "t_b")
+        for s in range(3):
+            wait("v", "mw%d" % s)
+            done(ts(T.sg[:, 40 * s:40 * s + 40], T.psw[:, 512 * s:512 * s + 40], 0.0, AluOpType.is_gt), "sg")
+        if t == 0:
+            wait("v", "t_b", "m_fb", "i_j")
+            done(V.tensor_copy(T.lp[:, 0:1], T.co[:, 128:129]), "k_l")
+            done(ts(T.lf[:], T.co[:, 160:224:32], fb, add), "k_l")
+            done(ts(T.jt[:], T.j0[:], h16, sub), "k_j")
+        wait("v", "sg", "m_mul2")
+        done(V.tensor_tensor_scan(T.sc[:], T.mul[:], T.sg[:], 0.0, mult, add), "sc")
+
+        wait("v", "sc")
+        for k in range(4):
+            o = 6 * (k % 2) + k // 2
+            done(ts(T.off1[:, o:o + 5:2], T.sc[:, 8 * k + 7:120:40], float(512 * (k // 2) + 16 * (k % 2)), add), "off1")
+        done(ts(T.offp[:, 1:6:2], T.sc[:, 39:120:40], float(Q3 + 16), add), "offp")
+        wait("v", "off1", "t_h1")
+        done(V.tensor_copy(T.g1[:], T.tab[:, Q0:Q0 + 1024].indirect(T.off1[:])), "g1")
+        wait("v", "k_l")
+        done(V.tensor_copy(T.offp[:, 6:22], T.sc[:].indirect(T.lp[:, 0:1])), "offp")
+        if t == 0:
+            done(V.transpose(T.tab[:, Q3:Q3 + 1024], T.inb[:, 1024:2048]), "t_h2")
+        wait("a", "offp", "t_h2", "t_h1", "i_id", "m_misc")
+        done(A.activation(T.gp[:], T.tab[:].indirect(T.offp[:, 0:18]), Copy), "gp")
+        done(A.activation(T.xp[:, EXT * 3 + C:EXT * 4], X[:, 3:1024:4], Copy), "xe_a")
+        wait("v", "g1")
+        done(V.transpose(T.t1[:], T.g1[:]), "t1")
+        wait("v", "t1")
+        done(V.tensor_tensor(T.a45[:], T.t1[:, 0:96:16], T.t1[:, 96:192:16], add), "a45")
+        done(V.tensor_tensor(T.a45v[:], T.t1[:, 8:96:16], T.t1[:, 96:192:16], add), "a45v")
+        wait("v", "a45")
+        done(ts(T.off2[:], T.a45[:], h16, add), "off2")
+        wait("v", "a45v", "k_j", "m_misc")
+        done(V.tensor_tensor(T.f[:, FA:FA + 6], T.a45v[:], T.jt[:, 0:6], add), "a45j")
+
+        wait("v", "off2", "t_h2")
+        done(V.tensor_copy(T.g2[:], T.tab[:, Q2:Q2 + 512].indirect(T.off2[:])), "g2")
+        wait("a", "a45j")
+        done(A.activation(T.f[64:128, FA - S1:FA - S1 + 6], T.f[0:64, FA:FA + 6], Copy), "mva1")
+        wait("a", "mva1")
+        done(A.activation(T.f[64:96, FA - S1 + S0:FA + S0 + 6], T.f[96:128, FA - S1:FA + 6], Copy), "mva2")
+        wait("v", "gp")
+        done(V.transpose(T.tp[:], T.gp[:]), "tp")
+        wait("v", "g2")
+        done(V.transpose(T.t2[:], T.g2[:]), "t2")
+        wait("v", "tp")
+        done(V.tensor_tensor(T.f[:, FE:FE + 18], T.tp[:, 0:288:16], T.jt[:], add), "vv")
+        wait("v", "t2")
+        for s in range(3):
+            done(ts(T.off3[:, 2 * s:2 * s + 2], T.t2[:, 32 * s:32 * s + 16:8], T.t2[:, 32 * s + 16:32 * s + 17], add), "off3")
+        wait("a", "vv")
+        done(A.activation(T.f[0:64, FV + S1:FV + S1 + 12], T.f[64:128, FV:FV + 12], Copy), "mvv1")
+        wait("a", "mvv1")
+        done(A.activation(T.f[0:32, FV + S0:FV + S0 + 24], T.f[32:64, FV:FV + 24], Copy), "mvv2")
+        done(A.activation(T.f[32:64, FV - S0:FV - S0 + 24], T.f[0:32, FV:FV + 24], Copy), "mvv2")
+
+        wait("v", "off3", "i_id")
+        done(V.tensor_copy(T.g3[:], T.tab[:, 0:2048].indirect(T.off3[:])), "g3")
+        wait("v", "g3")
+        done(V.transpose(T.t3[:], T.g3[:]), "t3")
+        wait("v", "t3", "vv")
+        for b in range(4):
+            o = FL + S1 * (b // 2) + S0 * (b % 2)
+            done(V.tensor_tensor(T.f[96:128, o:o + 6], T.t3[32 * b:32 * b + 32, 8:96:16],
+                                 T.f[32 * b:32 * b + 32, FE:FE + 6], add), "fin")
+        wait("v", "fin", "mva2", "mvv2")
+        done(V.tensor_copy(T.offz[:], T.f[:].indirect(T.lf[:])), "offz")
+
+        wait("v", "offz", "xm0", "xe_g")
+        wait("a", "offz", "xm2", "xe_a")
+        for b in range(2):
+            done(V.tensor_copy(T.z[:, b:4 * C:4], T.xp[:, EXT * b:EXT * (b + 1)].indirect(T.offz[:, 0:18])), "zg_v")
+            done(A.activation(T.z[:, b + 2:4 * C:4], T.xp[:, EXT * (b + 2):EXT * (b + 3)].indirect(T.offz[:, 0:18]), Copy), "zg_a")
+        done(V.tensor_copy(T.ld[:, 0:32], T.offz[:]), "ld")
+        wait("v", "zg_v", "zg_a")
+        done(V.quantize_mx(QZ[:], SZ[:], T.z[:]), "qz")
+        dst = T.cores[(rank + 1 + t) % N]
+        rid, pid = topo.addr(dst, core)
+        mask, ne = topo.mask(core, dst), len(topo.engines(core, dst))
+        arr = "arr%d" % t
+        wait("g", "qz")
+        g.remote_dma(QL[:].bitcast(dt.uint8), QZ[:].bitcast(dt.uint8), T.sem[arr], T.sem.sent, pid, rid, mask)
+        g.remote_dma(SL[:], SZ[:], T.sem[arr], T.sem.sent, pid, rid, mask)
+        cnt["sent"] = cnt.get("sent", 0) + 2 * ne
+        src = T.cores[(rank - 1 - t) % N]
+        cnt[arr] = 2 * len(topo.engines(src, core))
+
+        done(V.tensor_copy(T.ld[:, 32:64], T.offz[:]), "ld")
+        wait("v", "ld")
+        done(V.transpose(T.lt[:], T.ld[:]), "lt")
+        wait("v", "lt")
+        done(V.transpose(T.ls[:], T.lt[:, 16:48]), "ls")
+        wait("v", "ls")
+        done(ts(T.lm[:], T.ls[:, 0:18], float(C), AluOpType.is_ge, -float(C), mult), "lm")
+        wait("v", "lm")
+        done(V.tensor_tensor(T.ln[:], T.lm[:], T.ls[:, 0:18], add), "ln")
+        wait("v", "ln")
+        done(V.tensor_copy(T.offg[:], T.ln[:]), "offg")
+        if t == 0:
+            wait("v", "d_v")
+            done(V.quantize_mx(T.qv[:], T.sv[:], T.vt[:]), "q_v")
+            done(iota(T.im[:, 0:C], [[1, C]], 0), "i_im")
+            done(iota(T.im[:, C:EXT], [[1, EXT - C]], 0), "i_im")
+        if t == R - 1:
+            wait("a", "i_im")
+            done(A.activation(T.lrow[:], T.im[:].indirect(T.offz[:, 0:18]), Copy), "lrow")
+            wait("s", "lrow")
+            done(SY.dma_start(T.lo[:], T.lrow[0:128:16, :]), "d_out", 16)
+
+        wait("t", arr, "d_w")
+        for b in range(4):
+            done(PE.matmul_mx(T.psh[:, 512 * b:512 * b + C], T.qw[:, 128 * b:128 * b + 128], T.sw[:, 128 * b:128 * b + 128],
+                              QL[:], SL[:], True, True), "mh%d" % b)
+        for b in range(4):
+            wait("a", "mh%d" % b)
+            done(A.activation(T.h[:, C * b:C * b + C], T.psh[:, 512 * b:512 * b + C], Copy, scale=0.03125), "h%d" % b)
+        wait("v", "offg", "xm2", "qz")
+        for b in range(4):
+            wait("v", "h%d" % b)
+            done(V.tensor_tensor(XN[:, b:4 * C:4], T.h[:, C * b:C * b + C].indirect(T.offg[:]),
+                                 T.xp[:, EXT * b:EXT * b + C], add), "xn")
+
+    wait("v", "xn")
+    done(V.quantize_mx(T.qx[:, 0:C], T.sx[:, 0:C], T["x%d" % R][:]), "qx")
+    wait("t", "qx", "q_v")
+    done(PE.matmul_mx(T.psy[:, 0:C], T.qv[:], T.sv[:], T.qx[:, 0:C], T.sx[:, 0:C], True, True), "my")
+    wait("s", "qx")
+    wait("a", "qx")
+    done(SY.dma_start(T.oc[:], T.qx[:, 0:C].bitcast(dt.uint8)), "d_out", 16)
+    for k in range(4):
+        done((SY if k < 2 else A).dma_start(T.osc[4 * k:4 * k + 4, :], T.sx[32 * k:32 * k + 4, 0:C]), "d_out", 16)
+    wait("v", "my")
+    done(V.tensor_copy(T.yb[:], T.psy[:, 0:C]), "yb")
+    wait("a", "yb")
+    done(A.dma_start(T.y[:], T.yb[:]), "d_out", 16)
+    for n in cnt:
+        if most.get(n, 0) < cnt[n]:
+            wait("g", n)

@@ -1,6 +1,7 @@
 from concourse.mybir import dt, AluOpType, ActivationFunctionType
 
 C, R = 288, 3
+CA = 160
 EXT = 544
 F8, U8 = "float8_e4m3fn_x4", "uint8"
 IDN, Q0, Q3, Q2, ZERO = 0, 512, 1536, 2048, 2560
@@ -69,8 +70,9 @@ SEMAPHORES = (
        "k_col", "k_offu", "k_l", "k_j", "q_pad", "q_u", "q_v", "p_uc", "p_us", "c_b1", "c_b2", "c_in", "t_h1", "t_h2"]
     + ["qx", "mw0", "mw1", "mw2", "sg", "sc", "off1", "g1", "t1", "a45", "off2", "g2", "t2", "off3", "g3", "t3",
        "fin", "offz", "offp", "gp", "tp", "vv", "a45v", "a45j", "mva1", "mva2", "mvv1", "mvv2",
-       "xm0", "xm1", "xm2", "xm3", "xe_g", "xe_a", "zg_v", "zg_a", "qz", "ld", "lt", "ls", "lm", "ln", "offg",
-       "mh0", "mh1", "mh2", "mh3", "h0", "h1", "h2", "h3", "xn", "lrow", "my", "yb"]
+       "xm0", "xm2", "xe_g", "xe_a", "zg_v0", "zg_a0", "qz0", "zg_v1", "zg_a1", "qz1", "ld", "lt", "ls", "lm", "ln",
+       "offg", "off1b", "mh0", "mh1", "mh2", "mh3", "h0", "h1", "h2", "h3", "xn0", "xn1", "xn2", "xn3", "lrow",
+       "my", "my2", "yb"]
 )
 
 
@@ -172,20 +174,21 @@ def rank_program(g, core, T, topo):
     for t in range(R):
         X, XN = T["x%d" % t], T["x%d" % (t + 1)]
         QZ, SZ, QL, SL = (T[n % t] for n in ("qz%d", "sz%d", "ql%d", "sl%d"))
-        ready = "d_x" if t == 0 else "xn"
+        ready = ["d_x" if t == 0 else "xn%d" % b for b in range(4)]
 
-        wait("v", ready, "q_pad")
+        wait("v", ready[2], ready[3], "q_pad")
         done(V.quantize_mx(T.qx[:, 0:C], T.sx[:, 0:C], X[:]), "qx")
         wait("t", "qx", "p_uc", "p_us")
         for s in range(3):
             done(PE.matmul_mx(T.psw[:, 512 * s:512 * s + 128], T.qx[:, 128 * s:128 * s + 128],
                               T.sx[:, 128 * s:128 * s + 128], T.qu2[:], T.su2[:], True, True), "mw%d" % s)
-        wait("a", ready)
         for b in range(4):
+            wait("a", ready[b])
             done(A.activation(T.xp[:, EXT * b:EXT * b + C], X[:, b:4 * C:4], Copy), "xm%d" % (b // 2 * 2))
-        done(A.activation(T.xp[:, EXT * 2 + C:EXT * 3], X[:, 2:1024:4], Copy), "xe_a")
-        wait("g", ready)
+            if b == 2 and t > 0:
+                done(A.activation(T.xp[:, EXT * 2 + C:EXT * 3], X[:, 2:1024:4], Copy), "xe_a")
         for b in range(2):
+            wait("g", ready[b])
             done(g.affine_select(T.xp[:, EXT * b + C:EXT * (b + 1)], X[:, b:1024:4], [[0, 256]],
                                  AluOpType.is_ge, 0.0, 0, 0), "xe_g")
         if t == 0:
@@ -205,12 +208,15 @@ def rank_program(g, core, T, topo):
         done(V.tensor_tensor_scan(T.sc[:], T.mul[:], T.sg[:], 0.0, mult, add), "sc")
 
         wait("v", "sc")
-        for k in range(4):
+        for k in (1, 3, 0, 2):
             o = 6 * (k % 2) + k // 2
-            done(ts(T.off1[:, o:o + 5:2], T.sc[:, 8 * k + 7:120:40], float(512 * (k // 2) + 16 * (k % 2)), add), "off1")
+            done(ts(T.off1[:, o:o + 5:2], T.sc[:, 8 * k + 7:120:40], float(512 * (k // 2) + 16 * (k % 2)), add),
+                 "off1" if k % 2 == 0 else "off1b")
+        wait("a", "off1b", "t_h1")
+        done(A.activation(T.g1[:, 96:192], T.tab[:, Q0:Q0 + 1024].indirect(T.off1[:, 6:12]), Copy), "g1")
         done(ts(T.offp[:, 1:6:2], T.sc[:, 39:120:40], float(Q3 + 16), add), "offp")
         wait("v", "off1", "t_h1")
-        done(V.tensor_copy(T.g1[:], T.tab[:, Q0:Q0 + 1024].indirect(T.off1[:])), "g1")
+        done(V.tensor_copy(T.g1[:, 0:96], T.tab[:, Q0:Q0 + 1024].indirect(T.off1[:, 0:6])), "g1")
         wait("v", "k_l")
         done(V.tensor_copy(T.offp[:, 6:22], T.sc[:].indirect(T.lp[:, 0:1])), "offp")
         if t == 0:
@@ -218,6 +224,8 @@ def rank_program(g, core, T, topo):
         wait("a", "offp", "t_h2", "t_h1", "i_id", "m_misc")
         done(A.activation(T.gp[:], T.tab[:].indirect(T.offp[:, 0:18]), Copy), "gp")
         done(A.activation(T.xp[:, EXT * 3 + C:EXT * 4], X[:, 3:1024:4], Copy), "xe_a")
+        if t == 0:
+            done(A.activation(T.xp[:, EXT * 2 + C:EXT * 3], X[:, 2:1024:4], Copy), "xe_a")
         wait("v", "g1")
         done(V.transpose(T.t1[:], T.g1[:]), "t1")
         wait("v", "t1")
@@ -263,23 +271,26 @@ def rank_program(g, core, T, topo):
 
         wait("v", "offz", "xm0", "xe_g")
         wait("a", "offz", "xm2", "xe_a")
-        for b in range(2):
-            done(V.tensor_copy(T.z[:, b:4 * C:4], T.xp[:, EXT * b:EXT * (b + 1)].indirect(T.offz[:, 0:18])), "zg_v")
-            done(A.activation(T.z[:, b + 2:4 * C:4], T.xp[:, EXT * (b + 2):EXT * (b + 3)].indirect(T.offz[:, 0:18]), Copy), "zg_a")
-        done(V.tensor_copy(T.ld[:, 0:32], T.offz[:]), "ld")
-        wait("v", "zg_v", "zg_a")
-        done(V.quantize_mx(QZ[:], SZ[:], T.z[:]), "qz")
         dst = T.cores[(rank + 1 + t) % N]
         rid, pid = topo.addr(dst, core)
         mask, ne = topo.mask(core, dst), len(topo.engines(core, dst))
         arr = "arr%d" % t
-        wait("g", "qz")
-        g.remote_dma(QL[:].bitcast(dt.uint8), QZ[:].bitcast(dt.uint8), T.sem[arr], T.sem.sent, pid, rid, mask)
+        for i, (c0, c1) in enumerate(((0, CA), (CA, C))):
+            lst = T.offz[:, c0 // 16:c1 // 16]
+            for b in range(2):
+                done(V.tensor_copy(T.z[:, 4 * c0 + b:4 * c1:4], T.xp[:, EXT * b:EXT * (b + 1)].indirect(lst)), "zg_v%d" % i)
+                done(A.activation(T.z[:, 4 * c0 + b + 2:4 * c1:4], T.xp[:, EXT * (b + 2):EXT * (b + 3)].indirect(lst), Copy),
+                     "zg_a%d" % i)
+            wait("v", "zg_v%d" % i, "zg_a%d" % i)
+            done(V.quantize_mx(QZ[:, c0:c1], SZ[:, c0:c1], T.z[:, 4 * c0:4 * c1]), "qz%d" % i)
+            wait("g", "qz%d" % i)
+            g.remote_dma(QL[:, c0:c1].bitcast(dt.uint8), QZ[:, c0:c1].bitcast(dt.uint8), T.sem[arr], T.sem.sent, pid, rid, mask)
         g.remote_dma(SL[:], SZ[:], T.sem[arr], T.sem.sent, pid, rid, mask)
-        cnt["sent"] = cnt.get("sent", 0) + 2 * ne
+        cnt["sent"] = cnt.get("sent", 0) + 3 * ne
         src = T.cores[(rank - 1 - t) % N]
-        cnt[arr] = 2 * len(topo.engines(src, core))
+        cnt[arr] = 3 * len(topo.engines(src, core))
 
+        done(V.tensor_copy(T.ld[:, 0:32], T.offz[:]), "ld")
         done(V.tensor_copy(T.ld[:, 32:64], T.offz[:]), "ld")
         wait("v", "ld")
         done(V.transpose(T.lt[:], T.ld[:]), "lt")
@@ -309,23 +320,28 @@ def rank_program(g, core, T, topo):
         for b in range(4):
             wait("a", "mh%d" % b)
             done(A.activation(T.h[:, C * b:C * b + C], T.psh[:, 512 * b:512 * b + C], Copy, scale=0.03125), "h%d" % b)
-        wait("v", "offg", "xm2", "qz")
+        wait("v", "offg", "xm2", "qz0", "qz1")
         for b in range(4):
             wait("v", "h%d" % b)
+            if b >= 2:
+                wait("v", "xn%d" % (b - 2))
             done(V.tensor_tensor(XN[:, b:4 * C:4], T.h[:, C * b:C * b + C].indirect(T.offg[:]),
-                                 T.xp[:, EXT * b:EXT * b + C], add), "xn")
+                                 T.xp[:, EXT * b:EXT * b + C], add), "xn%d" % b)
 
-    wait("v", "xn")
+    wait("v", "xn2", "xn3")
     done(V.quantize_mx(T.qx[:, 0:C], T.sx[:, 0:C], T["x%d" % R][:]), "qx")
     wait("t", "qx", "q_v")
-    done(PE.matmul_mx(T.psy[:, 0:C], T.qv[:], T.sv[:], T.qx[:, 0:C], T.sx[:, 0:C], True, True), "my")
+    H = C // 2
+    done(PE.matmul_mx(T.psy[:, 0:H], T.qv[:], T.sv[:], T.qx[:, 0:H], T.sx[:, 0:H], True, True), "my")
+    done(PE.matmul_mx(T.psw[:, 0:H], T.qv[:], T.sv[:], T.qx[:, H:C], T.sx[:, H:C], True, True), "my2")
     wait("s", "qx")
-    wait("a", "qx")
     done(SY.dma_start(T.oc[:], T.qx[:, 0:C].bitcast(dt.uint8)), "d_out", 16)
     for k in range(4):
-        done((SY if k < 2 else A).dma_start(T.osc[4 * k:4 * k + 4, :], T.sx[32 * k:32 * k + 4, 0:C]), "d_out", 16)
-    wait("v", "my")
-    done(V.tensor_copy(T.yb[:], T.psy[:, 0:C]), "yb")
+        done(SY.dma_start(T.osc[4 * k:4 * k + 4, :], T.sx[32 * k:32 * k + 4, 0:C]), "d_out", 16)
+    wait("a", "my")
+    done(A.activation(T.yb[:, 0:H], T.psy[:, 0:H], Copy), "yb")
+    wait("v", "my2")
+    done(V.tensor_copy(T.yb[:, H:C], T.psw[:, 0:H]), "yb")
     wait("a", "yb")
     done(A.dma_start(T.y[:], T.yb[:]), "d_out", 16)
     for n in cnt:

from concourse.mybir import dt, AluOpType, ActivationFunctionType

C, R = 288, 3
CA = 160
EXT = 544
F8, U8 = "float8_e4m3fn_x4", "uint8"
IDN, Q0, Q3, Q2, ZERO = 0, 512, 1536, 2048, 2560
FE, FV, FA, FL = 30, 36, 108, 160
S1, S0 = 12, 32
FBASE = (FV, FV - S0 + 6, FA - S1, FL)

SCRATCH = {
    "xp": ("sbuf", [128, 4 * EXT], "bfloat16"),
    "z": ("sbuf", [128, 4 * C], "bfloat16"),
    "ut": ("sbuf", [128, 512], "bfloat16"),
    "vt": ("sbuf", [128, 512], "bfloat16"),
    "zt": ("sbuf", [128, 512], "bfloat16"),
    "qu": ("sbuf", [128, 128], F8), "su": ("sbuf", [128, 128], U8),
    "qu2": ("sbuf", [128, 128], F8), "su2": ("sbuf", [128, 128], U8),
    "qv": ("sbuf", [128, 128], F8), "sv": ("sbuf", [128, 128], U8),
    "qw": ("sbuf", [128, 512], F8), "sw": ("sbuf", [128, 512], U8),
    "qx": ("sbuf", [128, 384], F8), "sx": ("sbuf", [128, 384], U8),
    "cts": ("sbuf", [128, 64], "int32"),
    "inb": ("sbuf", [128, 2048], "bfloat16"),
    "tab": ("sbuf", [128, ZERO + 16], "bfloat16"),
    "ci": ("sbuf", [128, 224], "float32"),
    "co": ("sbuf", [128, 224], "float32"),
    "col": ("sbuf", [128, 8], "float32"),
    "j0": ("sbuf", [128, 18], "float32"),
    "jt": ("sbuf", [128, 18], "float32"),
    "im": ("sbuf", [128, EXT], "float32"),
    "mul": ("sbuf", [128, 120], "float32"),
    "sg": ("sbuf", [128, 120], "float32"),
    "sc": ("sbuf", [128, 120], "float32"),
    "offu": ("sbuf", [128, 8], "uint16"),
    "lp": ("sbuf", [128, 2], "uint16"),
    "lf": ("sbuf", [128, 2], "uint16"),
    "off1": ("sbuf", [128, 12], "uint16"),
    "off2": ("sbuf", [128, 6], "uint16"),
    "off3": ("sbuf", [128, 6], "uint16"),
    "offp": ("sbuf", [128, 22], "uint16"),
    "offz": ("sbuf", [128, 32], "uint16"),
    "offg": ("sbuf", [128, 18], "uint16"),
    "g1": ("sbuf", [128, 192], "bfloat16"), "t1": ("sbuf", [128, 192], "bfloat16"),
    "g2": ("sbuf", [128, 96], "bfloat16"), "t2": ("sbuf", [128, 96], "bfloat16"),
    "g3": ("sbuf", [128, 96], "bfloat16"), "t3": ("sbuf", [128, 96], "bfloat16"),
    "gp": ("sbuf", [128, 288], "bfloat16"), "tp": ("sbuf", [128, 288], "bfloat16"),
    "a45": ("sbuf", [128, 6], "float32"), "a45v": ("sbuf", [128, 6], "float32"),
    "f": ("sbuf", [128, 224], "float32"),
    "ld": ("sbuf", [128, 64], "float32"), "lt": ("sbuf", [128, 64], "float32"),
    "ls": ("sbuf", [128, 32], "float32"), "lm": ("sbuf", [128, 18], "float32"), "ln": ("sbuf", [128, 18], "float32"),
    "lrow": ("sbuf", [128, C], "float32"),
    "h": ("sbuf", [128, 4 * C], "float32"),
    "yb": ("sbuf", [128, C], "float32"),
    "psw": ("psum", [128, 1536], "float32"),
    "psh": ("psum", [128, 2048], "float32"),
    "psy": ("psum", [128, 512], "float32"),
}
for _t in range(R + 1):
    SCRATCH["x%d" % _t] = ("sbuf", [128, 4 * C], "bfloat16")
for _t in range(R):
    SCRATCH["qz%d" % _t] = ("sbuf", [128, C], F8)
    SCRATCH["sz%d" % _t] = ("sbuf", [128, C], U8)
    SCRATCH["ql%d" % _t] = ("sbuf", [128, C], F8)
    SCRATCH["sl%d" % _t] = ("sbuf", [128, C], U8)

SEMAPHORES = (
    ["d_x", "d_u", "d_v", "d_w", "d_ct", "d_out", "sent", "arr0", "arr1", "arr2"]
    + ["m_ci", "m_inb", "m_zt", "m_mul", "m_mul2", "m_misc", "m_fb", "i_a", "i_b", "i_j", "i_id", "i_im", "t_a", "t_b",
       "k_col", "k_offu", "k_l", "k_j", "q_pad", "q_u", "q_v", "p_uc", "p_us", "c_b1", "c_b2", "c_in", "t_h1", "t_h2"]
    + ["qx", "mw0", "mw1", "mw2", "sg", "sc", "off1", "g1", "t1", "a45", "off2", "g2", "t2", "off3", "g3", "t3",
       "fin", "offz", "offp", "gp", "tp", "vv", "a45v", "a45j", "mva1", "mva2", "mvv1", "mvv2",
       "xm0", "xm2", "xe_g", "xe_a", "zg_v0", "zg_a0", "qz0", "zg_v1", "zg_a1", "qz1", "ld", "lt", "ls", "lm", "ln",
       "offg", "off1b", "mh0", "mh1", "mh2", "mh3", "h0", "h1", "h2", "h3", "xn0", "xn1", "xn2", "xn3", "lrow",
       "my", "my2", "yb"]
)


def rank_program(g, core, T, topo):
    rank = T.rank_of(core)
    if rank is None:
        return
    N = len(T.cores)
    V, A, PE, SY = g.vector, g.scalar, g.tensor, g.sync
    Q = {"v": V, "a": A, "t": PE, "s": SY, "g": g}
    add, mult, sub = AluOpType.add, AluOpType.mult, AluOpType.subtract
    Copy = ActivationFunctionType.Copy
    cnt = {}
    seen = {}
    most = {}

    def wait(q, *names):
        for n in names:
            c = cnt[n]
            if seen.get((q, n), 0) < c:
                Q[q].wait_ge(T.sem[n], c)
                seen[(q, n)] = c
                most[n] = max(most.get(n, 0), c)

    def done(ins, name, k=1):
        ins.then_inc(T.sem[name], k)
        cnt[name] = cnt.get(name, 0) + k

    def ts(out, in0, s1, op0, s2=None, op1=None):
        if op1 is None:
            return V.tensor_scalar(out, in0, s1, None, op0)
        return V.tensor_scalar(out, in0, s1, s2, op0, op1)

    def iota(out, pattern, base, cm=0):
        return g.iota(out, pattern, base, cm, allow_small_or_imprecise_dtypes=True)

    done(SY.dma_start(T.x0[:], T.x[:]), "d_x", 16)
    done(A.dma_start(T.ut[:], T.u[:]), "d_u", 16)
    for i, q in enumerate((0, 1, 3, 2)):
        done(A.dma_start(T.cts[0:32, 16 * i:16 * i + 16], T.ct[32 * q:32 * q + 32, :]), "d_ct", 16)
    done(SY.dma_start(T.qw[:].bitcast(dt.uint8), T.wc[:]), "d_w", 16)
    done(SY.dma_start(T.sw[:], T.ws[:]), "d_w", 16)
    done(SY.dma_start(T.vt[:], T.v[:]), "d_v", 16)

    done(iota(T.ci[:, 0:32], [[0, 2], [16, 4], [1, 4]], 0), "i_a")
    done(iota(T.ci[:, 32:64], [[0, 2], [16, 4], [1, 4]], 64), "i_a")
    done(iota(T.ci[:, 64:96], [[0, 4], [-112, 2], [1, 4]], 112), "i_a")
    done(iota(T.ci[:, 96:128], [[1, 2], [0, 16]], 0), "i_a")
    done(V.memset(T.ci[:, 128:160], 0.0), "m_ci")
    done(V.memset(T.zt[:], 0.0), "m_zt")
    done(V.memset(T.mul[:], 2.0), "m_mul")
    done(V.memset(T.inb[:], 0.0), "m_inb")
    wait("g", "m_ci")
    for h in range(2):
        done(iota(T.ci[:, 128 + 16 * h:140 + 16 * h], [[16, 2], [40, 3], [8, 2]], 7), "i_b")
        for s in range(2):
            done(iota(T.ci[:, 160 + 16 * h + 8 * s:168 + 16 * h + 8 * s], [[S1, 2], [S0, 2], [1, 2]], 2 * s), "i_b")
    done(iota(T.ci[:, 192:224], [[0, 16], [1, 2]], 4), "i_b")
    done(iota(T.j0[:], [[0, 3], [128, 3], [16, 2]], 0, 1), "i_j")
    done(iota(T.tab[:, IDN:IDN + 512], [[16, 16], [0, 2], [1, 16]], 0), "i_id")

    wait("v", "m_zt", "m_mul")
    done(V.quantize_mx(T.qx[:, 256:384], T.sx[:, 256:384], T.zt[:]), "q_pad")
    done(V.memset(T.mul[:, 0:120:8], 0.0), "m_mul2")
    done(V.memset(T.mul[:, 4:120:8], 4.0), "m_mul2")
    done(V.memset(T.f[:], 0.0), "m_misc")
    done(V.memset(T.tab[:, ZERO:ZERO + 16], 0.0), "m_misc")
    done(V.memset(T.offp[:, 0:6:2], ZERO), "m_misc")
    done(V.memset(T.offu[:, 3:8], 0), "k_offu")
    for b in range(4):
        done(V.memset(T.col[32 * b:32 * b + 32, 4:5], float(FBASE[b])), "m_fb")
    wait("v", "i_a")
    done(V.transpose(T.co[:, 0:128], T.ci[:, 0:128]), "t_a")
    wait("v", "t_a")
    done(V.tensor_copy(T.offu[:, 0:3], T.co[:, 0:96:32]), "k_offu")
    odd = T.co[:, 96:97]
    done(ts(T.col[:, 0:1], odd, 16.0, mult), "k_col")
    done(ts(T.col[:, 1:2], odd, -31.0, mult, 32.0, add), "k_col")
    done(ts(T.col[:, 2:3], odd, -15.0, mult, 16.0, add), "k_col")
    done(ts(T.col[:, 3:4], odd, -float(Q3), mult, float(Q3), add), "k_col")
    h16, sA, sB, bB, fb = (T.col[:, i:i + 1] for i in range(5))

    wait("v", "d_u")
    done(V.quantize_mx(T.qu[:], T.su[:], T.ut[:]), "q_u")
    wait("v", "d_ct")
    done(V.tensor_copy(T.cts[32:64, :], T.cts[0:32, :]), "c_b1")
    wait("v", "q_u", "k_offu")
    done(V.tensor_copy(T.qu2[:].bitcast(dt.uint32), T.qu[:].bitcast(dt.uint32).indirect(T.offu[:])), "p_uc")
    wait("a", "q_u", "k_offu")
    done(A.activation(T.su2[:], T.su[:].indirect(T.offu[:]), Copy), "p_us")
    wait("v", "c_b1")
    done(V.tensor_copy(T.cts[64:128, :], T.cts[0:64, :]), "c_b2")
    wait("v", "c_b2", "k_col", "m_inb")
    for i in (0, 16):
        done(ts(T.inb[:, i:2048:32], T.cts[:], sA, mult), "c_in")
        done(ts(T.inb[:, i + 8:1536:32], T.cts[:, 0:48], sB, mult), "c_in")
        done(ts(T.inb[:, 1536 + i + 8:2048:32], T.cts[:, 48:64], sA, mult, bB, add), "c_in")

    for t in range(R):
        X, XN = T["x%d" % t], T["x%d" % (t + 1)]
        QZ, SZ, QL, SL = (T[n % t] for n in ("qz%d", "sz%d", "ql%d", "sl%d"))
        ready = ["d_x" if t == 0 else "xn%d" % b for b in range(4)]

        wait("v", ready[2], ready[3], "q_pad")
        done(V.quantize_mx(T.qx[:, 0:C], T.sx[:, 0:C], X[:]), "qx")
        wait("t", "qx", "p_uc", "p_us")
        for s in range(3):
            done(PE.matmul_mx(T.psw[:, 512 * s:512 * s + 128], T.qx[:, 128 * s:128 * s + 128],
                              T.sx[:, 128 * s:128 * s + 128], T.qu2[:], T.su2[:], True, True), "mw%d" % s)
        for b in range(4):
            wait("a", ready[b])
            done(A.activation(T.xp[:, EXT * b:EXT * b + C], X[:, b:4 * C:4], Copy), "xm%d" % (b // 2 * 2))
            if b == 2 and t > 0:
                done(A.activation(T.xp[:, EXT * 2 + C:EXT * 3], X[:, 2:1024:4], Copy), "xe_a")
        for b in range(2):
            wait("g", ready[b])
            done(g.affine_select(T.xp[:, EXT * b + C:EXT * (b + 1)], X[:, b:1024:4], [[0, 256]],
                                 AluOpType.is_ge, 0.0, 0, 0), "xe_g")
        if t == 0:
            wait("v", "c_in")
            done(V.transpose(T.tab[:, Q0:Q0 + 1024], T.inb[:, 0:1024]), "t_h1")
            wait("v", "i_b")
            done(V.transpose(T.co[:, 128:224], T.ci[:, 128:224]), "t_b")
        for s in range(3):
            wait("v", "mw%d" % s)
            done(ts(T.sg[:, 40 * s:40 * s + 40], T.psw[:, 512 * s:512 * s + 40], 0.0, AluOpType.is_gt), "sg")
        if t == 0:
            wait("v", "t_b", "m_fb", "i_j")
            done(V.tensor_copy(T.lp[:, 0:1], T.co[:, 128:129]), "k_l")
            done(ts(T.lf[:], T.co[:, 160:224:32], fb, add), "k_l")
            done(ts(T.jt[:], T.j0[:], h16, sub), "k_j")
        wait("v", "sg", "m_mul2")
        done(V.tensor_tensor_scan(T.sc[:], T.mul[:], T.sg[:], 0.0, mult, add), "sc")

        wait("v", "sc")
        for k in (1, 3, 0, 2):
            o = 6 * (k % 2) + k // 2
            done(ts(T.off1[:, o:o + 5:2], T.sc[:, 8 * k + 7:120:40], float(512 * (k // 2) + 16 * (k % 2)), add),
                 "off1" if k % 2 == 0 else "off1b")
        wait("a", "off1b", "t_h1")
        done(A.activation(T.g1[:, 96:192], T.tab[:, Q0:Q0 + 1024].indirect(T.off1[:, 6:12]), Copy), "g1")
        done(ts(T.offp[:, 1:6:2], T.sc[:, 39:120:40], float(Q3 + 16), add), "offp")
        wait("v", "off1", "t_h1")
        done(V.tensor_copy(T.g1[:, 0:96], T.tab[:, Q0:Q0 + 1024].indirect(T.off1[:, 0:6])), "g1")
        wait("v", "k_l")
        done(V.tensor_copy(T.offp[:, 6:22], T.sc[:].indirect(T.lp[:, 0:1])), "offp")
        if t == 0:
            done(V.transpose(T.tab[:, Q3:Q3 + 1024], T.inb[:, 1024:2048]), "t_h2")
        wait("a", "offp", "t_h2", "t_h1", "i_id", "m_misc")
        done(A.activation(T.gp[:], T.tab[:].indirect(T.offp[:, 0:18]), Copy), "gp")
        done(A.activation(T.xp[:, EXT * 3 + C:EXT * 4], X[:, 3:1024:4], Copy), "xe_a")
        if t == 0:
            done(A.activation(T.xp[:, EXT * 2 + C:EXT * 3], X[:, 2:1024:4], Copy), "xe_a")
        wait("v", "g1")
        done(V.transpose(T.t1[:], T.g1[:]), "t1")
        wait("v", "t1")
        done(V.tensor_tensor(T.a45[:], T.t1[:, 0:96:16], T.t1[:, 96:192:16], add), "a45")
        done(V.tensor_tensor(T.a45v[:], T.t1[:, 8:96:16], T.t1[:, 96:192:16], add), "a45v")
        wait("v", "a45")
        done(ts(T.off2[:], T.a45[:], h16, add), "off2")
        wait("v", "a45v", "k_j", "m_misc")
        done(V.tensor_tensor(T.f[:, FA:FA + 6], T.a45v[:], T.jt[:, 0:6], add), "a45j")

        wait("v", "off2", "t_h2")
        done(V.tensor_copy(T.g2[:], T.tab[:, Q2:Q2 + 512].indirect(T.off2[:])), "g2")
        wait("a", "a45j")
        done(A.activation(T.f[64:128, FA - S1:FA - S1 + 6], T.f[0:64, FA:FA + 6], Copy), "mva1")
        wait("a", "mva1")
        done(A.activation(T.f[64:96, FA - S1 + S0:FA + S0 + 6], T.f[96:128, FA - S1:FA + 6], Copy), "mva2")
        wait("v", "gp")
        done(V.transpose(T.tp[:], T.gp[:]), "tp")
        wait("v", "g2")
        done(V.transpose(T.t2[:], T.g2[:]), "t2")
        wait("v", "tp")
        done(V.tensor_tensor(T.f[:, FE:FE + 18], T.tp[:, 0:288:16], T.jt[:], add), "vv")
        wait("v", "t2")
        for s in range(3):
            done(ts(T.off3[:, 2 * s:2 * s + 2], T.t2[:, 32 * s:32 * s + 16:8], T.t2[:, 32 * s + 16:32 * s + 17], add), "off3")
        wait("a", "vv")
        done(A.activation(T.f[0:64, FV + S1:FV + S1 + 12], T.f[64:128, FV:FV + 12], Copy), "mvv1")
        wait("a", "mvv1")
        done(A.activation(T.f[0:32, FV + S0:FV + S0 + 24], T.f[32:64, FV:FV + 24], Copy), "mvv2")
        done(A.activation(T.f[32:64, FV - S0:FV - S0 + 24], T.f[0:32, FV:FV + 24], Copy), "mvv2")

        wait("v", "off3", "i_id")
        done(V.tensor_copy(T.g3[:], T.tab[:, 0:2048].indirect(T.off3[:])), "g3")
        wait("v", "g3")
        done(V.transpose(T.t3[:], T.g3[:]), "t3")
        wait("v", "t3", "vv")
        for b in range(4):
            o = FL + S1 * (b // 2) + S0 * (b % 2)
            done(V.tensor_tensor(T.f[96:128, o:o + 6], T.t3[32 * b:32 * b + 32, 8:96:16],
                                 T.f[32 * b:32 * b + 32, FE:FE + 6], add), "fin")
        wait("v", "fin", "mva2", "mvv2")
        done(V.tensor_copy(T.offz[:], T.f[:].indirect(T.lf[:])), "offz")

        wait("v", "offz", "xm0", "xe_g")
        wait("a", "offz", "xm2", "xe_a")
        dst = T.cores[(rank + 1 + t) % N]
        rid, pid = topo.addr(dst, core)
        mask, ne = topo.mask(core, dst), len(topo.engines(core, dst))
        arr = "arr%d" % t
        for i, (c0, c1) in enumerate(((0, CA), (CA, C))):
            lst = T.offz[:, c0 // 16:c1 // 16]
            for b in range(2):
                done(V.tensor_copy(T.z[:, 4 * c0 + b:4 * c1:4], T.xp[:, EXT * b:EXT * (b + 1)].indirect(lst)), "zg_v%d" % i)
                done(A.activation(T.z[:, 4 * c0 + b + 2:4 * c1:4], T.xp[:, EXT * (b + 2):EXT * (b + 3)].indirect(lst), Copy),
                     "zg_a%d" % i)
            wait("v", "zg_v%d" % i, "zg_a%d" % i)
            done(V.quantize_mx(QZ[:, c0:c1], SZ[:, c0:c1], T.z[:, 4 * c0:4 * c1]), "qz%d" % i)
            wait("g", "qz%d" % i)
            g.remote_dma(QL[:, c0:c1].bitcast(dt.uint8), QZ[:, c0:c1].bitcast(dt.uint8), T.sem[arr], T.sem.sent, pid, rid, mask)
        g.remote_dma(SL[:], SZ[:], T.sem[arr], T.sem.sent, pid, rid, mask)
        cnt["sent"] = cnt.get("sent", 0) + 3 * ne
        src = T.cores[(rank - 1 - t) % N]
        cnt[arr] = 3 * len(topo.engines(src, core))

        done(V.tensor_copy(T.ld[:, 0:32], T.offz[:]), "ld")
        done(V.tensor_copy(T.ld[:, 32:64], T.offz[:]), "ld")
        wait("v", "ld")
        done(V.transpose(T.lt[:], T.ld[:]), "lt")
        wait("v", "lt")
        done(V.transpose(T.ls[:], T.lt[:, 16:48]), "ls")
        wait("v", "ls")
        done(ts(T.lm[:], T.ls[:, 0:18], float(C), AluOpType.is_ge, -float(C), mult), "lm")
        wait("v", "lm")
        done(V.tensor_tensor(T.ln[:], T.lm[:], T.ls[:, 0:18], add), "ln")
        wait("v", "ln")
        done(V.tensor_copy(T.offg[:], T.ln[:]), "offg")
        if t == 0:
            wait("v", "d_v")
            done(V.quantize_mx(T.qv[:], T.sv[:], T.vt[:]), "q_v")
            done(iota(T.im[:, 0:C], [[1, C]], 0), "i_im")
            done(iota(T.im[:, C:EXT], [[1, EXT - C]], 0), "i_im")
        if t == R - 1:
            wait("a", "i_im")
            done(A.activation(T.lrow[:], T.im[:].indirect(T.offz[:, 0:18]), Copy), "lrow")
            wait("s", "lrow")
            done(SY.dma_start(T.lo[:], T.lrow[0:128:16, :]), "d_out", 16)

        wait("t", arr, "d_w")
        for b in range(4):
            done(PE.matmul_mx(T.psh[:, 512 * b:512 * b + C], T.qw[:, 128 * b:128 * b + 128], T.sw[:, 128 * b:128 * b + 128],
                              QL[:], SL[:], True, True), "mh%d" % b)
        for b in range(4):
            wait("a", "mh%d" % b)
            done(A.activation(T.h[:, C * b:C * b + C], T.psh[:, 512 * b:512 * b + C], Copy, scale=0.03125), "h%d" % b)
        wait("v", "offg", "xm2", "qz0", "qz1")
        for b in range(4):
            wait("v", "h%d" % b)
            if b >= 2:
                wait("v", "xn%d" % (b - 2))
            done(V.tensor_tensor(XN[:, b:4 * C:4], T.h[:, C * b:C * b + C].indirect(T.offg[:]),
                                 T.xp[:, EXT * b:EXT * b + C], add), "xn%d" % b)

    wait("v", "xn2", "xn3")
    done(V.quantize_mx(T.qx[:, 0:C], T.sx[:, 0:C], T["x%d" % R][:]), "qx")
    wait("t", "qx", "q_v")
    H = C // 2
    done(PE.matmul_mx(T.psy[:, 0:H], T.qv[:], T.sv[:], T.qx[:, 0:H], T.sx[:, 0:H], True, True), "my")
    done(PE.matmul_mx(T.psw[:, 0:H], T.qv[:], T.sv[:], T.qx[:, H:C], T.sx[:, H:C], True, True), "my2")
    wait("s", "qx")
    done(SY.dma_start(T.oc[:], T.qx[:, 0:C].bitcast(dt.uint8)), "d_out", 16)
    for k in range(4):
        done(SY.dma_start(T.osc[4 * k:4 * k + 4, :], T.sx[32 * k:32 * k + 4, 0:C]), "d_out", 16)
    wait("a", "my")
    done(A.activation(T.yb[:, 0:H], T.psy[:, 0:H], Copy), "yb")
    wait("v", "my2")
    done(V.tensor_copy(T.yb[:, H:C], T.psw[:, 0:H]), "yb")
    wait("a", "yb")
    done(A.dma_start(T.y[:], T.yb[:]), "d_out", 16)
    for n in cnt:
        if most.get(n, 0) < cnt[n]:
            wait("g", n)
